import numpy as np, ml_dtypes
CORES = [0,8,16,24,128,136,144,152,256,264,272,280,384,392,400,408]
N = 16
H = 4
ROWS, COLS = 4, 4
PERIODIC = True
def setup_inputs(rng):
    return {"x": rng.standard_normal((N, 128, 128), dtype=np.float32).astype(ml_dtypes.bfloat16)}
def reference(x):
    W = x.shape[2]
    y = np.zeros((N, 4, 128, H), x.dtype)
    for r in range(N):
        i, j = divmod(r, COLS)
        for k, (di, dj, cols) in enumerate([(-1, 0, slice(W - H, W)), (1, 0, slice(0, H)), (0, -1, slice(W - H, W)), (0, 1, slice(0, H))]):
            a, b = i + di, j + dj
            if PERIODIC:
                a, b = a % ROWS, b % COLS
            if 0 <= a < ROWS and 0 <= b < COLS:
                y[r][k] = x[a * COLS + b][:, cols]
    return {"y": y}

@@ -1,0 +1,70 @@
+from concourse.bass import DstId, RemoteDMATransfer
+
+SCRATCH = {
+    "edge": ("dram", [2, 128, 4], "bfloat16"),
+    "hold": ("dram", [128, 4], "bfloat16"),
+    "land": ("dram", [4, 128, 4], "bfloat16"),
+}
+SEMAPHORES = ["loaded", "arrived", "sent", "stored"]
+
+ROWS, COLS, W, HALO = 4, 4, 128, 4
+E = 2
+M_FAR, M_UP, M_DOWN = 0x03, 0x0C, 0x30
+M_NEAR = 0x300
+M_RELAY = 0x03
+
+
+def routes(T):
+    out = []
+    for r, src in enumerate(T.cores):
+        i, j = divmod(r, COLS)
+        for dj, e, slot in ((-1, 0, 3), (1, 1, 2)):
+            d = (j + dj) % COLS
+            dst = T.cores[i * COLS + d]
+            if d == j ^ 1:
+                relay = src + 2
+            else:
+                relay = T.cores[i * COLS + (d ^ 1)] + 3
+            out.append((src, relay, dst, e, slot))
+    return out
+
+
+def rank_program(g, core, T, topo):
+    sem = T.sem
+    table = routes(T)
+
+    def tr(dst_core, dst_ap, src_ap, mask):
+        rid, pid = topo.addr(dst_core, core)
+        return RemoteDMATransfer(dst_ids=[DstId(rid=rid, pnc=pid)], dma_engine_mask=mask, remote_sem=sem.arrived,
+                                 src=src_ap, dst=dst_ap)
+
+    rank = T.rank_of(core)
+    if rank is None:
+        for src, relay, dst, e, slot in table:
+            if relay == core:
+                g.wait_ge(sem.arrived, E)
+                rid, pid = topo.addr(dst, core)
+                g.remote_dma(T.land[slot], T.hold[:], sem.arrived, sem.sent, pid, rid, M_RELAY)
+                g.wait_ge(sem.sent, E)
+        return
+
+    i, j = divmod(rank, COLS)
+    g.dma_start(T.edge[0], T.x[:, 0:HALO]).then_inc(sem.loaded, 16)
+    g.dma_start(T.edge[1], T.x[:, W - HALO:W]).then_inc(sem.loaded, 16)
+    g.wait_ge(sem.loaded, 32)
+
+    feed = []
+    for src, relay, dst, e, slot in table:
+        if src == core:
+            feed.append(tr(relay, T.hold[:], T.edge[e], M_NEAR if relay == core + 2 else M_FAR))
+    g.remote_dma_fused(feed, local_sem=sem.sent)
+
+    up = T.cores[((i - 1) % ROWS) * COLS + j]
+    down = T.cores[((i + 1) % ROWS) * COLS + j]
+    g.remote_dma_fused([tr(up, T.land[1], T.edge[0], M_UP), tr(down, T.land[0], T.edge[1], M_DOWN)],
+                       local_sem=sem.sent)
+
+    g.wait_ge(sem.arrived, 4 * E)
+    g.dma_start(T.y[:], T.land[:]).then_inc(sem.stored, 16)
+    g.wait_ge(sem.sent, 4 * E)
+    g.wait_ge(sem.stored, 16)

@@ -5,7 +5,7 @@ SCRATCH = {
     "hold": ("dram", [128, 4], "bfloat16"),
     "land": ("dram", [4, 128, 4], "bfloat16"),
 }
-SEMAPHORES = ["loaded", "arrived", "sent", "stored"]
+SEMAPHORES = ["loaded_far", "loaded_near", "arrived", "sent", "stored"]
 
 ROWS, COLS, W, HALO = 4, 4, 128, 4
 E = 2
@@ -49,15 +49,20 @@ def rank_program(g, core, T, topo):
         return
 
     i, j = divmod(rank, COLS)
-    g.dma_start(T.edge[0], T.x[:, 0:HALO]).then_inc(sem.loaded, 16)
-    g.dma_start(T.edge[1], T.x[:, W - HALO:W]).then_inc(sem.loaded, 16)
-    g.wait_ge(sem.loaded, 32)
+    mine = [t for t in table if t[0] == core]
+    far = [t for t in mine if t[1] != core + 2][0]
+    near = [t for t in mine if t[1] == core + 2][0]
+    cols = (slice(0, HALO), slice(W - HALO, W))
 
-    feed = []
-    for src, relay, dst, e, slot in table:
-        if src == core:
-            feed.append(tr(relay, T.hold[:], T.edge[e], M_NEAR if relay == core + 2 else M_FAR))
-    g.remote_dma_fused(feed, local_sem=sem.sent)
+    g.dma_start(T.edge[far[3]], T.x[:, cols[far[3]]]).then_inc(sem.loaded_far, 16)
+    g.dma_start(T.edge[near[3]], T.x[:, cols[near[3]]]).then_inc(sem.loaded_near, 16)
+
+    g.wait_ge(sem.loaded_far, 16)
+    rid, pid = topo.addr(far[1], core)
+    g.remote_dma(T.hold[:], T.edge[far[3]], sem.arrived, sem.sent, pid, rid, M_FAR)
+    g.wait_ge(sem.loaded_near, 16)
+    rid, pid = topo.addr(near[1], core)
+    g.remote_dma(T.hold[:], T.edge[near[3]], sem.arrived, sem.sent, pid, rid, M_NEAR)
 
     up = T.cores[((i - 1) % ROWS) * COLS + j]
     down = T.cores[((i + 1) % ROWS) * COLS + j]

@@ -8,10 +8,13 @@ SCRATCH = {
 SEMAPHORES = ["loaded_far", "loaded_near", "arrived", "sent", "stored"]
 
 ROWS, COLS, W, HALO = 4, 4, 128, 4
-E = 2
-M_FAR, M_UP, M_DOWN = 0x03, 0x0C, 0x30
-M_NEAR = 0x300
+M_FAR, M_VFAR = 0x03, 0x0C
+M_NEAR, M_VNEAR = 0x300, 0x30
 M_RELAY = 0x03
+
+
+def engines(mask):
+    return bin(mask).count("1")
 
 
 def routes(T):
@@ -42,10 +45,10 @@ def rank_program(g, core, T, topo):
     if rank is None:
         for src, relay, dst, e, slot in table:
             if relay == core:
-                g.wait_ge(sem.arrived, E)
+                g.wait_ge(sem.arrived, engines(M_NEAR if relay == src + 2 else M_FAR))
                 rid, pid = topo.addr(dst, core)
                 g.remote_dma(T.land[slot], T.hold[:], sem.arrived, sem.sent, pid, rid, M_RELAY)
-                g.wait_ge(sem.sent, E)
+                g.wait_ge(sem.sent, engines(M_RELAY))
         return
 
     i, j = divmod(rank, COLS)
@@ -57,19 +60,20 @@ def rank_program(g, core, T, topo):
     g.dma_start(T.edge[far[3]], T.x[:, cols[far[3]]]).then_inc(sem.loaded_far, 16)
     g.dma_start(T.edge[near[3]], T.x[:, cols[near[3]]]).then_inc(sem.loaded_near, 16)
 
-    g.wait_ge(sem.loaded_far, 16)
-    rid, pid = topo.addr(far[1], core)
-    g.remote_dma(T.hold[:], T.edge[far[3]], sem.arrived, sem.sent, pid, rid, M_FAR)
-    g.wait_ge(sem.loaded_near, 16)
-    rid, pid = topo.addr(near[1], core)
-    g.remote_dma(T.hold[:], T.edge[near[3]], sem.arrived, sem.sent, pid, rid, M_NEAR)
-
     up = T.cores[((i - 1) % ROWS) * COLS + j]
     down = T.cores[((i + 1) % ROWS) * COLS + j]
-    g.remote_dma_fused([tr(up, T.land[1], T.edge[0], M_UP), tr(down, T.land[0], T.edge[1], M_DOWN)],
+    vert = ((up, 1), (down, 0))
+
+    g.wait_ge(sem.loaded_far, 16)
+    v, slot = vert[far[3]]
+    g.remote_dma_fused([tr(far[1], T.hold[:], T.edge[far[3]], M_FAR), tr(v, T.land[slot], T.edge[far[3]], M_VFAR)],
+                       local_sem=sem.sent)
+    g.wait_ge(sem.loaded_near, 16)
+    v, slot = vert[near[3]]
+    g.remote_dma_fused([tr(near[1], T.hold[:], T.edge[near[3]], M_NEAR), tr(v, T.land[slot], T.edge[near[3]], M_VNEAR)],
                        local_sem=sem.sent)
 
-    g.wait_ge(sem.arrived, 4 * E)
+    g.wait_ge(sem.arrived, 2 * engines(M_RELAY) + engines(M_VFAR) + engines(M_VNEAR))
     g.dma_start(T.y[:], T.land[:]).then_inc(sem.stored, 16)
-    g.wait_ge(sem.sent, 4 * E)
+    g.wait_ge(sem.sent, engines(M_FAR) + engines(M_VFAR) + engines(M_NEAR) + engines(M_VNEAR))
     g.wait_ge(sem.stored, 16)

from concourse.bass import DstId, RemoteDMATransfer

SCRATCH = {
    "edge": ("dram", [2, 128, 4], "bfloat16"),
    "hold": ("dram", [128, 4], "bfloat16"),
    "land": ("dram", [4, 128, 4], "bfloat16"),
}
SEMAPHORES = ["loaded_far", "loaded_near", "arrived", "sent", "stored"]

ROWS, COLS, W, HALO = 4, 4, 128, 4
M_FAR, M_VFAR = 0x03, 0x0C
M_NEAR, M_VNEAR = 0x300, 0x30
M_RELAY = 0x03


def engines(mask):
    return bin(mask).count("1")


def routes(T):
    out = []
    for r, src in enumerate(T.cores):
        i, j = divmod(r, COLS)
        for dj, e, slot in ((-1, 0, 3), (1, 1, 2)):
            d = (j + dj) % COLS
            dst = T.cores[i * COLS + d]
            if d == j ^ 1:
                relay = src + 2
            else:
                relay = T.cores[i * COLS + (d ^ 1)] + 3
            out.append((src, relay, dst, e, slot))
    return out


def rank_program(g, core, T, topo):
    sem = T.sem
    table = routes(T)

    def tr(dst_core, dst_ap, src_ap, mask):
        rid, pid = topo.addr(dst_core, core)
        return RemoteDMATransfer(dst_ids=[DstId(rid=rid, pnc=pid)], dma_engine_mask=mask, remote_sem=sem.arrived,
                                 src=src_ap, dst=dst_ap)

    rank = T.rank_of(core)
    if rank is None:
        for src, relay, dst, e, slot in table:
            if relay == core:
                g.wait_ge(sem.arrived, engines(M_NEAR if relay == src + 2 else M_FAR))
                rid, pid = topo.addr(dst, core)
                g.remote_dma(T.land[slot], T.hold[:], sem.arrived, sem.sent, pid, rid, M_RELAY)
                g.wait_ge(sem.sent, engines(M_RELAY))
        return

    i, j = divmod(rank, COLS)
    mine = [t for t in table if t[0] == core]
    far = [t for t in mine if t[1] != core + 2][0]
    near = [t for t in mine if t[1] == core + 2][0]
    cols = (slice(0, HALO), slice(W - HALO, W))

    g.dma_start(T.edge[far[3]], T.x[:, cols[far[3]]]).then_inc(sem.loaded_far, 16)
    g.dma_start(T.edge[near[3]], T.x[:, cols[near[3]]]).then_inc(sem.loaded_near, 16)

    up = T.cores[((i - 1) % ROWS) * COLS + j]
    down = T.cores[((i + 1) % ROWS) * COLS + j]
    vert = ((up, 1), (down, 0))

    g.wait_ge(sem.loaded_far, 16)
    v, slot = vert[far[3]]
    g.remote_dma_fused([tr(far[1], T.hold[:], T.edge[far[3]], M_FAR), tr(v, T.land[slot], T.edge[far[3]], M_VFAR)],
                       local_sem=sem.sent)
    g.wait_ge(sem.loaded_near, 16)
    v, slot = vert[near[3]]
    g.remote_dma_fused([tr(near[1], T.hold[:], T.edge[near[3]], M_NEAR), tr(v, T.land[slot], T.edge[near[3]], M_VNEAR)],
                       local_sem=sem.sent)

    g.wait_ge(sem.arrived, 2 * engines(M_RELAY) + engines(M_VFAR) + engines(M_VNEAR))
    g.dma_start(T.y[:], T.land[:]).then_inc(sem.stored, 16)
    g.wait_ge(sem.sent, engines(M_FAR) + engines(M_VFAR) + engines(M_NEAR) + engines(M_VNEAR))
    g.wait_ge(sem.stored, 16)
